import numpy as np
import ml_dtypes


def mxq(x, axis, fmt="e4m3"):
    dtype, down = {"e4m3": (ml_dtypes.float8_e4m3fn, 7), "e5m2": (ml_dtypes.float8_e5m2, 14)}[fmt]
    v = np.moveaxis(np.asarray(x, np.float32).astype(ml_dtypes.bfloat16).astype(np.float64), axis, -1)
    blocks = v.reshape(v.shape[:-1] + (-1, 32))
    amax = np.abs(blocks).max(-1, keepdims=True)
    byte = np.maximum(np.where(amax > 0, np.frexp(amax)[1] - 1 + 127, 0) - down, 1)
    scale = np.exp2(byte - 127.0)
    codes = (blocks / scale).astype(np.float32).astype(dtype).astype(np.float64)
    return np.moveaxis((codes * scale).reshape(v.shape), -1, axis)


WIDE = False


def mx_kscale(k):
    if not WIDE:
        return np.ones(k)
    levels = np.array([10, -10, 5, -5, 0])
    if k % 512:
        return np.exp2(np.random.permutation(np.resize(levels, k // 32))).repeat(32)
    a = np.empty((k // 512, 16))
    for p in range(k // 512):
        a[p, :8] = np.random.permutation(np.resize(levels, 8))
        for g in range(8):
            far = levels[np.abs(levels - a[p, g]) >= 10]
            a[p, g + 8] = far[np.random.randint(len(far))]
    return np.exp2(a.ravel()).repeat(32)


def f64(x):
    return np.asarray(x).astype(np.float64)


def striped(idx):
    return np.tile(idx.reshape(-1, 16).T, (8, 1)).astype(np.uint16)


def unstriped(offs):
    return offs[:16].T.reshape(-1).astype(np.int64)


E2M1 = np.array([0.0, 0.5, 1.0, 1.5, 2.0, 3.0, 4.0, 6.0, -0.0, -0.5, -1.0, -1.5, -2.0, -3.0, -4.0, -6.0])


def pack_weight(w, fmt):
    k, n = w.shape
    w = f64(np.asarray(w, np.float32).astype(ml_dtypes.bfloat16)).reshape(k // 32, 32, n)
    amax = np.abs(w).max(1)
    if fmt == "e4m3":
        byte = np.frexp(amax)[1] - 1 + 127 - 7
    else:
        mant, ex = np.frexp(amax / 6.0)
        byte = np.where(mant > 0.5, ex, ex - 1) + 127
    byte = np.clip(np.where(amax > 0, byte, 1), 1, 254)
    scaled = (w * np.exp2(127.0 - byte)[:, None, :]).reshape(k, n).astype(np.float32)
    by_word = np.ascontiguousarray(scaled.reshape(k // 512, 128, 4, n).transpose(0, 1, 3, 2))
    if fmt == "e4m3":
        words = by_word.astype(ml_dtypes.float8_e4m3fn).view(np.uint8)
    else:
        c = by_word.astype(ml_dtypes.float4_e2m1fn).view(np.uint8) & 0xF
        words = (c[..., 0::2] | (c[..., 1::2] << 4)).reshape(k // 512, 128, 2 * n)
    return np.ascontiguousarray(words), np.ascontiguousarray(byte.astype(np.uint8).reshape(k // 512, 16, n))


def unpack_weight(words, scales, fmt):
    g, _, n = scales.shape
    words = np.ascontiguousarray(words).reshape(g, 128, n, -1)
    if fmt == "e4m3":
        vals = words.view(ml_dtypes.float8_e4m3fn).astype(np.float64)
    else:
        nib = np.empty((g, 128, n, 4), np.uint8)
        nib[..., 0::2] = words & 0xF
        nib[..., 1::2] = words >> 4
        vals = E2M1[nib]
    vals = vals * np.repeat(np.exp2(scales.astype(np.float64) - 127.0), 8, axis=1)[..., None]
    return vals.transpose(0, 1, 3, 2).reshape(g * 512, n)


def gelu(v):
    return 0.5 * v * (1.0 + np.tanh(np.sqrt(2.0 / np.pi) * (v + 0.044715 * v**3)))


def bf(x):
    return np.asarray(x, np.float32).astype(ml_dtypes.bfloat16)


def planes(Y):
    n, m = Y.shape
    b = f64(bf(Y)).reshape(n // 32, 32, m)
    amax = np.abs(b).max(1)
    byte = np.clip(np.where(amax > 0, np.frexp(amax)[1] - 1 + 127 - 7, 1), 1, 254)
    codes = (b * np.exp2(127.0 - byte)[:, None, :]).reshape(n, m).astype(np.float32).astype(ml_dtypes.float8_e4m3fn).view(np.uint8)
    words = codes.reshape(n // 512, 128, 4, m).transpose(0, 1, 3, 2)
    return np.ascontiguousarray(words), np.ascontiguousarray(byte.astype(np.uint8).reshape(n // 512, 16, m))


K, H, N, T, S, P = 1024, 1024, 512, 4096, 1024, 512

def setup_inputs():
    n = np.random.standard_normal
    s = mx_kscale(K)[:, None]
    u = mx_kscale(H)[:, None]
    spread = np.exp(0.8 * n(N))[None, :]
    d = {}
    d["tab_words"], d["tab_scales"] = pack_weight(n((K, T)) * s, "e2m1")
    d["offs"] = striped(np.random.permutation(T)[:S])
    d["pos1"] = striped(np.random.permutation(S)[:P])
    d["pos2"] = striped(np.random.permutation(S)[:P])
    d["w1"] = (1.6 * n((K, H)) / K ** 0.5 / s).astype(np.float32)
    d["gain"] = (np.exp(0.4 * n(H)) * u[:, 0]).astype(np.float32)
    d["wa"] = (0.4 * n((H, N)) / H ** 0.5 / u * spread).astype(np.float32)
    d["wb_words"], d["wb_scales"] = pack_weight(1.0 * n((H, N)) / H ** 0.5 / u * spread, "e2m1")
    d["wc_words"], d["wc_scales"] = pack_weight(0.3 * n((H, N)) / H ** 0.5 / u * spread, "e4m3")
    return d

def reference(tab_words, tab_scales, offs, pos1, pos2, w1, gain, wa, wb_words, wb_scales, wc_words, wc_scales):
    v = unpack_weight(tab_words, tab_scales, "e2m1")[:, unstriped(offs)]
    wb = unpack_weight(wb_words, wb_scales, "e2m1")
    wc = unpack_weight(wc_words, wc_scales, "e4m3")
    gr = f64(gain)[:, None]
    f = mxq(f64(w1), 0, "e4m3").T @ v
    h = gr * f
    left = h[:, unstriped(pos1)]
    bent = gr * np.tanh(f[:, unstriped(pos2)])
    diff = np.abs(left - h[:, unstriped(pos2)])
    ql = mxq(left, 0, "e4m3")
    qb = mxq(bent, 0, "e4m3")
    qd = mxq(diff, 0, "e4m3")
    y = mxq(f64(wa), 0, "e4m3").T @ ql + wb.T @ qb + wc.T @ qd
    words, scales = planes(y)
    return y, words, scales

@@ -1,0 +1,277 @@
+from contextlib import ExitStack
+
+import concourse.mybir as mybir
+
+K, H, N, T, S, PAIRS = 1024, 1024, 512, 4096, 1024, 512
+FLOPS = 2 * K * H * S + 3 * 2 * H * N * PAIRS
+
+F32 = mybir.dt.float32
+BF16 = mybir.dt.bfloat16
+I32 = mybir.dt.int32
+U32 = mybir.dt.uint32
+U16 = mybir.dt.uint16
+U8 = mybir.dt.uint8
+FP8X4 = mybir.dt.float8_e4m3fn_x4
+FP4X4 = mybir.dt.float4_e2m1fn_x4
+ACT = mybir.ActivationFunctionType
+ALU = mybir.AluOpType
+
+P = 128
+PACK = 4
+PASS = P * PACK
+BANK = 512
+QUARTER = 128
+CHUNKS = ((0, 0, 512), (1, 0, 256), (1, 256, 128), (1, 384, 128))
+
+
+def tile_list_otolith_pair_features_kernel(
+    tc, tab_words, tab_scales, offs, pos1, pos2, w1, gain, wa, wb_words, wb_scales, wc_words, wc_scales,
+    out_0, out_1, out_2,
+):
+    nc = tc.nc
+    with ExitStack() as ctx:
+        lists = ctx.enter_context(tc.tile_pool(name="lists", bufs=1))
+        keep = ctx.enter_context(tc.tile_pool(name="keep", bufs=1))
+        stage = ctx.enter_context(tc.tile_pool(name="stage", bufs=3))
+        f_psum = ctx.enter_context(tc.psum_pool(name="f_psum", bufs=4))
+        y_psum = ctx.enter_context(tc.psum_pool(name="y_psum", bufs=1))
+
+        offs_sb = lists.tile([P, S // 16], U16, name="offs_sb")
+        pos1_sb = lists.tile([P, PAIRS // 16], U16, name="pos1_sb")
+        pos2_sb = lists.tile([P, PAIRS // 16], U16, name="pos2_sb")
+
+        tab_scale_win = keep.tile([P, T], U8, name="tab_scale_win", tag="scale_rows", align_bytes=64)
+        nc.vector.memset(tab_scale_win[:].bitcast(I32), 0)
+        v_scale1 = keep.tile([P, S], U8, name="v_scale1", align_bytes=64)
+        nc.vector.memset(v_scale1[:].bitcast(I32), 0)
+        for r in range(4):
+            nc.scalar.dma_start(
+                out=tab_scale_win[r:P:16, :].bitcast(I32),
+                in_=tab_scales.rearrange("a (q r) t -> r q a t", r=4)[r].bitcast(I32),
+            )
+        gain_sb = keep.tile([P, 2, PACK], F32, name="gain_sb")
+
+        def load_rows(w, row0, col0, width, name, tag):
+            raw = keep.tile([P, PACK, width], F32, name="raw_" + name, tag=tag, align_bytes=64)
+            nc.sync.dma_start(
+                out=raw[:],
+                in_=w[row0 : row0 + PASS, col0 : col0 + width].rearrange("(p j) c -> p j c", j=PACK),
+            )
+            return raw
+
+        def cast_rows(engine, grouped, raw, m0):
+            width = raw.shape[2]
+            dst = grouped[:].rearrange("p (t m j) -> p m j t", t=PACK, j=PACK)[:, m0 : m0 + width // PACK]
+            src = raw[:].rearrange("p j (m t) -> p m j t", t=PACK)
+            if engine == "scalar":
+                nc.scalar.copy(out=dst, in_=src)
+            else:
+                nc.vector.tensor_copy(out=dst, in_=src)
+
+        def quantize(grouped, name):
+            width = grouped.shape[1] // PACK
+            codes = keep.tile([P, width], U32, name=name + "_codes", align_bytes=64)
+            scales = keep.tile([P, width], U8, name=name + "_scales", align_bytes=64)
+            nc.vector.quantize_mx(out=codes[:].bitcast(FP8X4), scales=scales[:], in_=grouped[:])
+            return codes, scales
+
+        def weight_group(name):
+            return stage.tile([P, PASS * PACK], BF16, name=name, tag="grouped", bufs=2, align_bytes=64)
+
+        nc.sync.dma_start(offs_sb[:], offs)
+        nc.sync.dma_start(pos2_sb[:], pos2)
+        nc.sync.dma_start(pos1_sb[:], pos1)
+        nc.sync.dma_start(out=gain_sb[:], in_=gain.rearrange("(b p t) -> p b t", b=2, t=PACK))
+        tab_win = []
+        for a in range(2):
+            tab_win.append(keep.tile([P, T], U16, name="tab_win%d" % a, tag="words%d" % a, align_bytes=64))
+        nc.sync.dma_start(out=tab_win[0][:].bitcast(I32), in_=tab_words[0].bitcast(I32))
+        raw00 = load_rows(w1, 0, 0, PASS, "w00", "rows_a")
+        nc.sync.dma_start(out=tab_win[1][:].bitcast(I32), in_=tab_words[1].bitcast(I32))
+        raw10 = [load_rows(w1, PASS, c, PASS // 2, "w10_%d" % c, "half%d" % c) for c in (0, PASS // 2)]
+
+        v_words = [keep.tile([P, S], U16, name="v_words%d" % a, align_bytes=64) for a in range(2)]
+        v_scale0 = keep.tile([P, S], U8, name="v_scale0", align_bytes=64)
+        nc.vector.tensor_copy(v_words[0][:], tab_win[0][:].indirect(offs_sb[:]))
+        nc.vector.tensor_copy(v_scale0[:], tab_scale_win[:].indirect(offs_sb[:]))
+        nc.sync.dma_start(out=v_scale1[0:112, :].bitcast(I32), in_=v_scale0[16:P, :].bitcast(I32))
+        nc.vector.tensor_copy(v_words[1][:], tab_win[1][:].indirect(offs_sb[:]))
+        v_scales = (v_scale0, v_scale1)
+
+        w1_q = {}
+        grouped = weight_group("g00")
+        cast_rows("scalar", grouped, raw00, 0)
+        w1_q[0, 0] = quantize(grouped, "w00")
+        grouped = weight_group("g10")
+        cast_rows("scalar", grouped, raw10[0], 0)
+        cast_rows("vector", grouped, raw10[1], P // 2)
+        w1_q[1, 0] = quantize(grouped, "w10")
+
+        inv_gain = keep.tile([P, 2, PACK], F32, name="inv_gain")
+        safe_gain = keep.tile([P, 2, PACK], F32, name="safe_gain")
+        nc.vector.scalar_tensor_tensor(
+            out=safe_gain[:], in0=gain_sb[:], scalar=0.0, in1=gain_sb[:], op0=ALU.is_equal, op1=ALU.add
+        )
+        nc.vector.reciprocal(out=inv_gain[:], in_=safe_gain[:])
+
+        h = {}
+
+        def stage1(b, t):
+            h[b, t] = keep.tile([P, S], F32, name="h%d%d" % (b, t))
+            banks = [f_psum.tile([P, BANK], F32, name="f_bank") for half in range(2)]
+            cols = slice(t * P, (t + 1) * P)
+            for a in range(2):
+                codes, scales = w1_q[a, b]
+                for half in range(2):
+                    m = slice(half * BANK, (half + 1) * BANK)
+                    nc.tensor.matmul_mx(
+                        out=banks[half][:],
+                        lhsT=codes[:, cols].bitcast(FP8X4),
+                        lhsT_scale=scales[:, cols],
+                        rhs=v_words[a][:, m].bitcast(FP4X4),
+                        rhs_scale=v_scales[a][:, m],
+                        start=(a == 0),
+                        stop=(a == 1),
+                    )
+            for half in range(2):
+                nc.scalar.activation(
+                    out=h[b, t][:, half * BANK : (half + 1) * BANK], in_=banks[half][:], func=ACT.Copy,
+                    scale=gain_sb[:, b, t : t + 1],
+                )
+
+        for t in range(PACK):
+            stage1(0, t)
+
+        raw01 = load_rows(w1, 0, PASS, PASS, "w01", "scale_rows")
+        raw11 = load_rows(w1, PASS, PASS, PASS, "w11", "rows_a")
+        for a, raw in ((0, raw01), (1, raw11)):
+            grouped = weight_group("g%d1" % a)
+            cast_rows("scalar", grouped, raw, 0)
+            w1_q[a, 1] = quantize(grouped, "w%d1" % a)
+        for t in range(PACK):
+            stage1(1, t)
+
+        wc_raw = keep.tile([P, 2, N], I32, name="wc_raw", tag="words1", align_bytes=64)
+        nc.sync.dma_start(out=wc_raw[:], in_=wc_words.rearrange("a p c i -> p a (c i)").bitcast(I32))
+        wb_raw = keep.tile([P, 2, N], U16, name="wb_raw", tag="half0", align_bytes=64)
+        nc.sync.dma_start(out=wb_raw[:].bitcast(I32), in_=wb_words.rearrange("a p c -> p a c").bitcast(I32))
+        wbc_rows = keep.tile([P, 2, N], U8, name="wbc_rows", tag="half256", align_bytes=64)
+        nc.vector.memset(wbc_rows[:].bitcast(I32), 0)
+        for k, rows in ((0, wb_scales), (4, wc_scales)):
+            for q in range(4):
+                nc.sync.dma_start(
+                    out=wbc_rows[32 * q + k : 32 * q + k + 4].bitcast(I32),
+                    in_=rows[:, 4 * q : 4 * q + 4, :].rearrange("a r c -> r a c").bitcast(I32),
+                )
+        wa_q = []
+        for b in range(2):
+            raw = load_rows(wa, b * PASS, 0, N, "wa%d" % b, ("scale_rows", "rows_a")[b])
+            grouped = weight_group("ga%d" % b)
+            cast_rows("scalar", grouped, raw, 0)
+            wa_q.append(quantize(grouped, "wa%d" % b))
+
+        wc_codes = keep.tile([P, 2, N], I32, name="wc_codes", align_bytes=64)
+        nc.vector.tensor_copy(
+            out=wc_codes[:].rearrange("p a (t c i) -> p a c t i", t=PACK, i=4),
+            in_=wc_raw[:].rearrange("p a (c i t) -> p a c t i", t=PACK, i=4),
+        )
+        wb_codes = keep.tile([P, 2, N], U16, name="wb_codes", align_bytes=64)
+        nc.vector.tensor_copy(
+            out=wb_codes[:].rearrange("p a (t m) -> p a t m", t=PACK),
+            in_=wb_raw[:].rearrange("p a (m t) -> p a t m", t=PACK),
+        )
+        wbc_scales = keep.tile([P, 2, N], U8, name="wbc_scales", align_bytes=64)
+        nc.vector.tensor_copy(
+            out=wbc_scales[:].rearrange("p a (t m) -> p a t m", t=PACK),
+            in_=wbc_rows[:].rearrange("p a (m t) -> p a t m", t=PACK),
+        )
+
+        def stationary(which, b, t):
+            cols = slice(t * P, (t + 1) * P)
+            if which == "left":
+                return wa_q[b][0][:, cols].bitcast(FP8X4), wa_q[b][1][:, cols]
+            if which == "bent":
+                return wb_codes[:, b, cols].bitcast(FP4X4), wbc_scales[:, b, cols]
+            return wc_codes[:, b, cols].bitcast(FP8X4), wbc_scales[4:P, b, cols]
+
+        y_banks = [y_psum.tile([P, PACK, QUARTER], F32, name="y_bank%d" % q) for q in range(PAIRS // QUARTER)]
+        y_codes = keep.tile([P, PAIRS], U32, name="y_codes", align_bytes=64)
+        y_scales = keep.tile([P, PAIRS], U8, name="y_scales", align_bytes=64)
+        y_rows = out_0.rearrange("(p t) j -> p t j", t=PACK)
+        y_words = out_1[0].rearrange("p m t -> p (m t)").bitcast(I32)
+
+        def walk_src(ap):
+            return ap.rearrange("p t (c i) -> p c t i", i=4)
+
+        def walk_dst(ap):
+            return ap.rearrange("p (c i t) -> p c t i", i=4, t=PACK)
+
+        def stage2(which, b, j0, operand):
+            codes, scales = operand
+            for c0 in range(0, codes.shape[1], QUARTER):
+                bank = y_banks[(j0 + c0) // QUARTER]
+                for t in range(PACK):
+                    lhsT, lhsT_scale = stationary(which, b, t)
+                    nc.tensor.matmul_mx(
+                        out=bank[:, t, :],
+                        lhsT=lhsT,
+                        lhsT_scale=lhsT_scale,
+                        rhs=codes[:, c0 : c0 + QUARTER].bitcast(FP8X4),
+                        rhs_scale=scales[:, c0 : c0 + QUARTER],
+                        start=(b == 0 and which == "bent" and t == 0),
+                        stop=(b == 1 and which == "diff" and t == PACK - 1),
+                    )
+
+        def finish(q):
+            j = slice(q * QUARTER, (q + 1) * QUARTER)
+            y = keep.tile([P, PACK, QUARTER], F32, name="y%d" % q, tag="y", bufs=2)
+            nc.scalar.copy(out=y[:], in_=y_banks[q][:])
+            nc.sync.dma_start(out=y_rows[:, :, j], in_=y[:])
+            y_grouped = keep.tile([P, PACK * QUARTER], BF16, name="y_grouped%d" % q, tag="y_grouped", bufs=2, align_bytes=64)
+            nc.vector.tensor_copy(out=walk_dst(y_grouped[:]), in_=walk_src(y[:]))
+            nc.vector.quantize_mx(out=y_codes[:, j].bitcast(FP8X4), scales=y_scales[:, j], in_=y_grouped[:])
+            nc.sync.dma_start(out=y_words[:, j], in_=y_codes[:, j].bitcast(I32))
+
+        for n, (b, j0, width) in enumerate(CHUNKS):
+            entries = slice(j0 // 16, (j0 + width) // 16)
+            h1 = keep.tile([P, PACK, width], F32, name="h1_%d" % n)
+            h2 = keep.tile([P, PACK, width], F32, name="h2_%d" % n)
+            bounded = keep.tile([P, PACK, width], F32, name="bounded_%d" % n)
+            gap = keep.tile([P, PACK, width], F32, name="gap_%d" % n)
+            left = keep.tile([P, PACK * width], BF16, name="left_%d" % n, align_bytes=64)
+            bent = keep.tile([P, PACK * width], BF16, name="bent_%d" % n, align_bytes=64)
+            diff = keep.tile([P, PACK * width], BF16, name="diff_%d" % n, align_bytes=64)
+            if b == 0:
+                bent_rows = keep.tile([P, PACK, width], BF16, name="bent_rows")
+            order = [(w, t) for t in range(PACK) for w in (2, 1)] if b == 0 else [(w, t) for w in (2, 1) for t in range(PACK)]
+            for w, t in order:
+                if w == 2:
+                    nc.vector.tensor_copy(h2[:, t, :], h[b, t][:].indirect(pos2_sb[:, entries]))
+                    nc.scalar.activation(
+                        out=bounded[:, t, :], in_=h2[:, t, :], func=ACT.Tanh, scale=inv_gain[:, b, t : t + 1]
+                    )
+                    if b == 0:
+                        nc.scalar.activation(
+                            out=bent_rows[:, t, :], in_=bounded[:, t, :], func=ACT.Copy, scale=gain_sb[:, b, t : t + 1]
+                        )
+                else:
+                    nc.vector.tensor_copy(h1[:, t, :], h[b, t][:].indirect(pos1_sb[:, entries]))
+            nc.vector.tensor_tensor(out=gap[:], in0=h1[:], in1=h2[:], op=ALU.subtract)
+            nc.scalar.copy(out=walk_dst(left[:]), in_=walk_src(h1[:]))
+            nc.scalar.activation(out=walk_dst(diff[:]), in_=walk_src(gap[:]), func=ACT.Abs)
+            if b == 0:
+                nc.scalar.copy(out=walk_dst(bent[:]), in_=walk_src(bent_rows[:]))
+            else:
+                gains = gain_sb[:, b, :].unsqueeze(1).unsqueeze(3).to_broadcast([P, width // 4, PACK, 4])
+                nc.vector.tensor_tensor(out=walk_dst(bent[:]), in0=walk_src(bounded[:]), in1=gains, op=ALU.mult)
+            for which, grouped in (("bent", bent), ("left", left), ("diff", diff)):
+                stage2(which, b, j0, quantize(grouped, "%s_%d" % (which, n)))
+            if b == 1:
+                for q in range(j0 // QUARTER, (j0 + width) // QUARTER):
+                    finish(q)
+
+        for q in range(4):
+            engine = nc.sync if q % 2 == 0 else nc.scalar
+            engine.dma_start(
+                out=out_2[0, 4 * q : 4 * q + 4, :].bitcast(I32), in_=y_scales[32 * q : 32 * q + 4, :].bitcast(I32)
+            )

@@ -21,7 +21,17 @@ PACK = 4
 PASS = P * PACK
 BANK = 512
 QUARTER = 128
-CHUNKS = ((0, 0, 512), (1, 0, 256), (1, 256, 128), (1, 384, 128))
+CHUNKS = ((0, 0, 256), (0, 256, 256), (1, 0, 256), (1, 256, 128), (1, 384, 128))
+H2_SLOTS = ("a2", "slot0", "a2", "slot0", "a2")
+H1_SLOTS = ("a1", "slot1", "a1", "slot1", "a1")
+T_MAJOR = (0, 2)
+SCALAR_COLS = 224
+BENT_SCALAR = ()
+WEAVE_SCALAR = ()
+GAP_G = ()
+BENT_G = ()
+Y_SCALAR = (0,)
+WA_ENG = ("scalar", "scalar")
 
 
 def tile_list_otolith_pair_features_kernel(
@@ -41,9 +51,9 @@ def tile_list_otolith_pair_features_kernel(
         pos2_sb = lists.tile([P, PAIRS // 16], U16, name="pos2_sb")
 
         tab_scale_win = keep.tile([P, T], U8, name="tab_scale_win", tag="scale_rows", align_bytes=64)
-        nc.vector.memset(tab_scale_win[:].bitcast(I32), 0)
+        nc.gpsimd.memset(tab_scale_win[:].bitcast(I32), 0)
         v_scale1 = keep.tile([P, S], U8, name="v_scale1", align_bytes=64)
-        nc.vector.memset(v_scale1[:].bitcast(I32), 0)
+        nc.gpsimd.memset(v_scale1[:].bitcast(I32), 0)
         for r in range(4):
             nc.scalar.dma_start(
                 out=tab_scale_win[r:P:16, :].bitcast(I32),
@@ -62,33 +72,44 @@ def tile_list_otolith_pair_features_kernel(
         def cast_rows(engine, grouped, raw, m0):
             width = raw.shape[2]
             dst = grouped[:].rearrange("p (t m j) -> p m j t", t=PACK, j=PACK)[:, m0 : m0 + width // PACK]
-            src = raw[:].rearrange("p j (m t) -> p m j t", t=PACK)
+            src = raw.rearrange("p j (m t) -> p m j t", t=PACK)
             if engine == "scalar":
                 nc.scalar.copy(out=dst, in_=src)
+            elif engine == "gpsimd":
+                for m in range(0, width // PACK, 32):
+                    nc.gpsimd.tensor_scalar(
+                        out=dst[:, m : m + 32], in0=src[:, m : m + 32], scalar1=1.0, scalar2=0.0, op0=ALU.mult, op1=ALU.add
+                    )
             else:
                 nc.vector.tensor_copy(out=dst, in_=src)
 
-        def quantize(grouped, name):
+        def quantize(grouped, name, parts=1):
             width = grouped.shape[1] // PACK
             codes = keep.tile([P, width], U32, name=name + "_codes", align_bytes=64)
             scales = keep.tile([P, width], U8, name=name + "_scales", align_bytes=64)
-            nc.vector.quantize_mx(out=codes[:].bitcast(FP8X4), scales=scales[:], in_=grouped[:])
+            step = width // parts
+            for c in range(0, width, step):
+                nc.vector.quantize_mx(
+                    out=codes[:, c : c + step].bitcast(FP8X4),
+                    scales=scales[:, c : c + step],
+                    in_=grouped[:, PACK * c : PACK * (c + step)],
+                )
             return codes, scales
 
-        def weight_group(name):
-            return stage.tile([P, PASS * PACK], BF16, name=name, tag="grouped", bufs=2, align_bytes=64)
+        def weight_group(name, tag):
+            return keep.tile([P, PASS * PACK], BF16, name=name, tag=tag, align_bytes=64)
 
         nc.sync.dma_start(offs_sb[:], offs)
-        nc.sync.dma_start(pos2_sb[:], pos2)
-        nc.sync.dma_start(pos1_sb[:], pos1)
         nc.sync.dma_start(out=gain_sb[:], in_=gain.rearrange("(b p t) -> p b t", b=2, t=PACK))
         tab_win = []
         for a in range(2):
             tab_win.append(keep.tile([P, T], U16, name="tab_win%d" % a, tag="words%d" % a, align_bytes=64))
         nc.sync.dma_start(out=tab_win[0][:].bitcast(I32), in_=tab_words[0].bitcast(I32))
+        nc.sync.dma_start(pos2_sb[:], pos2)
+        nc.sync.dma_start(pos1_sb[:], pos1)
         raw00 = load_rows(w1, 0, 0, PASS, "w00", "rows_a")
         nc.sync.dma_start(out=tab_win[1][:].bitcast(I32), in_=tab_words[1].bitcast(I32))
-        raw10 = [load_rows(w1, PASS, c, PASS // 2, "w10_%d" % c, "half%d" % c) for c in (0, PASS // 2)]
+        raw10 = load_rows(w1, PASS, 0, PASS, "w10", "rows_b")
 
         v_words = [keep.tile([P, S], U16, name="v_words%d" % a, align_bytes=64) for a in range(2)]
         v_scale0 = keep.tile([P, S], U8, name="v_scale0", align_bytes=64)
@@ -99,13 +120,13 @@ def tile_list_otolith_pair_features_kernel(
         v_scales = (v_scale0, v_scale1)
 
         w1_q = {}
-        grouped = weight_group("g00")
-        cast_rows("scalar", grouped, raw00, 0)
+        grouped = weight_group("g00", "slot0")
+        cast_rows("scalar", grouped, raw00[:], 0)
         w1_q[0, 0] = quantize(grouped, "w00")
-        grouped = weight_group("g10")
-        cast_rows("scalar", grouped, raw10[0], 0)
-        cast_rows("vector", grouped, raw10[1], P // 2)
-        w1_q[1, 0] = quantize(grouped, "w10")
+        grouped = weight_group("g10", "slot1")
+        cast_rows("scalar", grouped, raw10[:, :, 0:SCALAR_COLS], 0)
+        cast_rows("vector", grouped, raw10[:, :, SCALAR_COLS:PASS], SCALAR_COLS // PACK)
+        w1_q[1, 0] = quantize(grouped, "w10", PACK)
 
         inv_gain = keep.tile([P, 2, PACK], F32, name="inv_gain")
         safe_gain = keep.tile([P, 2, PACK], F32, name="safe_gain")
@@ -134,57 +155,57 @@ def tile_list_otolith_pair_features_kernel(
                         stop=(a == 1),
                     )
             for half in range(2):
-                nc.scalar.activation(
-                    out=h[b, t][:, half * BANK : (half + 1) * BANK], in_=banks[half][:], func=ACT.Copy,
-                    scale=gain_sb[:, b, t : t + 1],
-                )
+                dst = h[b, t][:, half * BANK : (half + 1) * BANK]
+                if (b, t, half) == (0, 0, 1):
+                    nc.vector.tensor_scalar(
+                        out=dst, in0=banks[half][:], scalar1=gain_sb[:, b, t : t + 1], scalar2=None, op0=ALU.mult
+                    )
+                else:
+                    nc.scalar.activation(out=dst, in_=banks[half][:], func=ACT.Copy, scale=gain_sb[:, b, t : t + 1])
 
-        for t in range(PACK):
-            stage1(0, t)
+        wa_q = {}
 
-        raw01 = load_rows(w1, 0, PASS, PASS, "w01", "scale_rows")
-        raw11 = load_rows(w1, PASS, PASS, PASS, "w11", "rows_a")
-        for a, raw in ((0, raw01), (1, raw11)):
-            grouped = weight_group("g%d1" % a)
-            cast_rows("scalar", grouped, raw, 0)
+        def first_weights(a):
+            raw = load_rows(w1, a * PASS, PASS, PASS, "w%d1" % a, ("scale_rows", "rows_a")[a])
+            grouped = weight_group("g%d1" % a, "slot%d" % a)
+            cast_rows("scalar", grouped, raw[:], 0)
             w1_q[a, 1] = quantize(grouped, "w%d1" % a)
-        for t in range(PACK):
-            stage1(1, t)
 
-        wc_raw = keep.tile([P, 2, N], I32, name="wc_raw", tag="words1", align_bytes=64)
-        nc.sync.dma_start(out=wc_raw[:], in_=wc_words.rearrange("a p c i -> p a (c i)").bitcast(I32))
-        wb_raw = keep.tile([P, 2, N], U16, name="wb_raw", tag="half0", align_bytes=64)
-        nc.sync.dma_start(out=wb_raw[:].bitcast(I32), in_=wb_words.rearrange("a p c -> p a c").bitcast(I32))
-        wbc_rows = keep.tile([P, 2, N], U8, name="wbc_rows", tag="half256", align_bytes=64)
-        nc.vector.memset(wbc_rows[:].bitcast(I32), 0)
-        for k, rows in ((0, wb_scales), (4, wc_scales)):
-            for q in range(4):
-                nc.sync.dma_start(
-                    out=wbc_rows[32 * q + k : 32 * q + k + 4].bitcast(I32),
-                    in_=rows[:, 4 * q : 4 * q + 4, :].rearrange("a r c -> r a c").bitcast(I32),
-                )
-        wa_q = []
-        for b in range(2):
+        def left_weights(b):
             raw = load_rows(wa, b * PASS, 0, N, "wa%d" % b, ("scale_rows", "rows_a")[b])
-            grouped = weight_group("ga%d" % b)
-            cast_rows("scalar", grouped, raw, 0)
-            wa_q.append(quantize(grouped, "wa%d" % b))
+            grouped = weight_group("ga%d" % b, "slot_wa")
+            cast_rows(WA_ENG[b], grouped, raw[:], 0)
+            wa_q[b] = quantize(grouped, "wa%d" % b)
 
         wc_codes = keep.tile([P, 2, N], I32, name="wc_codes", align_bytes=64)
-        nc.vector.tensor_copy(
-            out=wc_codes[:].rearrange("p a (t c i) -> p a c t i", t=PACK, i=4),
-            in_=wc_raw[:].rearrange("p a (c i t) -> p a c t i", t=PACK, i=4),
-        )
         wb_codes = keep.tile([P, 2, N], U16, name="wb_codes", align_bytes=64)
-        nc.vector.tensor_copy(
-            out=wb_codes[:].rearrange("p a (t m) -> p a t m", t=PACK),
-            in_=wb_raw[:].rearrange("p a (m t) -> p a t m", t=PACK),
-        )
         wbc_scales = keep.tile([P, 2, N], U8, name="wbc_scales", align_bytes=64)
-        nc.vector.tensor_copy(
-            out=wbc_scales[:].rearrange("p a (t m) -> p a t m", t=PACK),
-            in_=wbc_rows[:].rearrange("p a (m t) -> p a t m", t=PACK),
-        )
+
+        def packed_weights():
+            wc_raw = keep.tile([P, 2, N], I32, name="wc_raw", tag="words1", align_bytes=64)
+            nc.sync.dma_start(out=wc_raw[:], in_=wc_words.rearrange("a p c i -> p a (c i)").bitcast(I32))
+            wb_raw = keep.tile([P, 2, N], U16, name="wb_raw", tag="rows_b", align_bytes=64)
+            nc.sync.dma_start(out=wb_raw[:].bitcast(I32), in_=wb_words.rearrange("a p c -> p a c").bitcast(I32))
+            nc.vector.tensor_copy(
+                out=wb_codes[:].rearrange("p a (t m) -> p a t m", t=PACK),
+                in_=wb_raw[:].rearrange("p a (m t) -> p a t m", t=PACK),
+            )
+            wbc_rows = keep.tile([P, 2, N], U8, name="wbc_rows", tag="rows_b", align_bytes=64)
+            nc.gpsimd.memset(wbc_rows[:].bitcast(I32), 0)
+            for k, rows in ((0, wb_scales), (4, wc_scales)):
+                for q in range(4):
+                    nc.sync.dma_start(
+                        out=wbc_rows[32 * q + k : 32 * q + k + 4].bitcast(I32),
+                        in_=rows[:, 4 * q : 4 * q + 4, :].rearrange("a r c -> r a c").bitcast(I32),
+                    )
+            nc.vector.tensor_copy(
+                out=wc_codes[:].rearrange("p a (t c i) -> p a c t i", t=PACK, i=4),
+                in_=wc_raw[:].rearrange("p a (c i t) -> p a c t i", t=PACK, i=4),
+            )
+            nc.vector.tensor_copy(
+                out=wbc_scales[:].rearrange("p a (t m) -> p a t m", t=PACK),
+                in_=wbc_rows[:].rearrange("p a (m t) -> p a t m", t=PACK),
+            )
 
         def stationary(which, b, t):
             cols = slice(t * P, (t + 1) * P)
@@ -228,47 +249,88 @@ def tile_list_otolith_pair_features_kernel(
             nc.scalar.copy(out=y[:], in_=y_banks[q][:])
             nc.sync.dma_start(out=y_rows[:, :, j], in_=y[:])
             y_grouped = keep.tile([P, PACK * QUARTER], BF16, name="y_grouped%d" % q, tag="y_grouped", bufs=2, align_bytes=64)
-            nc.vector.tensor_copy(out=walk_dst(y_grouped[:]), in_=walk_src(y[:]))
+            if q in Y_SCALAR:
+                nc.scalar.copy(out=walk_dst(y_grouped[:]), in_=walk_src(y[:]))
+            else:
+                nc.vector.tensor_copy(out=walk_dst(y_grouped[:]), in_=walk_src(y[:]))
             nc.vector.quantize_mx(out=y_codes[:, j].bitcast(FP8X4), scales=y_scales[:, j], in_=y_grouped[:])
             nc.sync.dma_start(out=y_words[:, j], in_=y_codes[:, j].bitcast(I32))
 
-        for n, (b, j0, width) in enumerate(CHUNKS):
+        picked = {}
+        GAP_ENG = lambda n: nc.gpsimd if n in GAP_G else nc.vector
+        BENT_ENG = lambda n: nc.gpsimd if n in BENT_G else nc.vector
+
+        def pick(n):
+            b, j0, width = CHUNKS[n]
             entries = slice(j0 // 16, (j0 + width) // 16)
-            h1 = keep.tile([P, PACK, width], F32, name="h1_%d" % n)
-            h2 = keep.tile([P, PACK, width], F32, name="h2_%d" % n)
-            bounded = keep.tile([P, PACK, width], F32, name="bounded_%d" % n)
-            gap = keep.tile([P, PACK, width], F32, name="gap_%d" % n)
-            left = keep.tile([P, PACK * width], BF16, name="left_%d" % n, align_bytes=64)
-            bent = keep.tile([P, PACK * width], BF16, name="bent_%d" % n, align_bytes=64)
-            diff = keep.tile([P, PACK * width], BF16, name="diff_%d" % n, align_bytes=64)
-            if b == 0:
-                bent_rows = keep.tile([P, PACK, width], BF16, name="bent_rows")
-            order = [(w, t) for t in range(PACK) for w in (2, 1)] if b == 0 else [(w, t) for w in (2, 1) for t in range(PACK)]
+            h2 = keep.tile([P, PACK, width], F32, name="h2_%d" % n, tag=H2_SLOTS[n], align_bytes=64)
+            h1 = keep.tile([P, PACK, width], F32, name="h1_%d" % n, tag=H1_SLOTS[n], align_bytes=64)
+            order = [(w, t) for t in range(PACK) for w in (2, 1)] if n in T_MAJOR else [(w, t) for w in (2, 1) for t in range(PACK)]
             for w, t in order:
-                if w == 2:
-                    nc.vector.tensor_copy(h2[:, t, :], h[b, t][:].indirect(pos2_sb[:, entries]))
-                    nc.scalar.activation(
-                        out=bounded[:, t, :], in_=h2[:, t, :], func=ACT.Tanh, scale=inv_gain[:, b, t : t + 1]
-                    )
-                    if b == 0:
-                        nc.scalar.activation(
-                            out=bent_rows[:, t, :], in_=bounded[:, t, :], func=ACT.Copy, scale=gain_sb[:, b, t : t + 1]
-                        )
-                else:
-                    nc.vector.tensor_copy(h1[:, t, :], h[b, t][:].indirect(pos1_sb[:, entries]))
-            nc.vector.tensor_tensor(out=gap[:], in0=h1[:], in1=h2[:], op=ALU.subtract)
+                dst, pos = (h2, pos2_sb) if w == 2 else (h1, pos1_sb)
+                nc.vector.tensor_copy(dst[:, t, :], h[b, t][:].indirect(pos[:, entries]))
+            gap = stage.tile([P, PACK, width], F32, name="gap_%d" % n, tag="gap", bufs=2)
+            GAP_ENG(n).tensor_tensor(out=gap[:], in0=h1[:], in1=h2[:], op=ALU.subtract)
+            picked[n] = (h1, h2, gap)
+
+        made = {}
+
+        def combine(n):
+            b, j0, width = CHUNKS[n]
+            h1, h2, gap = picked[n]
+            bounded = stage.tile([P, PACK, width], F32, name="bounded_%d" % n, tag="bounded", bufs=2)
+            left = stage.tile([P, PACK * width], BF16, name="left_%d" % n, tag="left", bufs=2, align_bytes=64)
+            bent = stage.tile([P, PACK * width], BF16, name="bent_%d" % n, tag="bent", bufs=2, align_bytes=64)
+            diff = stage.tile([P, PACK * width], BF16, name="diff_%d" % n, tag="diff", bufs=2, align_bytes=64)
+            for t in range(PACK):
+                nc.scalar.activation(
+                    out=bounded[:, t, :], in_=h2[:, t, :], func=ACT.Tanh, scale=inv_gain[:, b, t : t + 1]
+                )
             nc.scalar.copy(out=walk_dst(left[:]), in_=walk_src(h1[:]))
             nc.scalar.activation(out=walk_dst(diff[:]), in_=walk_src(gap[:]), func=ACT.Abs)
-            if b == 0:
-                nc.scalar.copy(out=walk_dst(bent[:]), in_=walk_src(bent_rows[:]))
+            if n in BENT_SCALAR:
+                rows = stage.tile([P, PACK, width], BF16, name="bent_rows_%d" % n, tag="bent_rows", bufs=2)
+                for t in range(PACK):
+                    nc.scalar.activation(out=rows[:, t, :], in_=bounded[:, t, :], func=ACT.Copy, scale=gain_sb[:, b, t : t + 1])
+                if n in WEAVE_SCALAR:
+                    nc.scalar.copy(out=walk_dst(bent[:]), in_=walk_src(rows[:]))
+                else:
+                    nc.vector.tensor_copy(out=walk_dst(bent[:]), in_=walk_src(rows[:]))
             else:
                 gains = gain_sb[:, b, :].unsqueeze(1).unsqueeze(3).to_broadcast([P, width // 4, PACK, 4])
-                nc.vector.tensor_tensor(out=walk_dst(bent[:]), in0=walk_src(bounded[:]), in1=gains, op=ALU.mult)
-            for which, grouped in (("bent", bent), ("left", left), ("diff", diff)):
-                stage2(which, b, j0, quantize(grouped, "%s_%d" % (which, n)))
+                BENT_ENG(n).tensor_tensor(out=walk_dst(bent[:]), in0=walk_src(bounded[:]), in1=gains, op=ALU.mult)
+            made[n] = [(which, quantize(grouped, "%s_%d" % (which, n))) for which, grouped in (("bent", bent), ("left", left), ("diff", diff))]
+
+        def multiply(n):
+            b, j0, width = CHUNKS[n]
+            for which, operand in made[n]:
+                stage2(which, b, j0, operand)
             if b == 1:
                 for q in range(j0 // QUARTER, (j0 + width) // QUARTER):
                     finish(q)
+
+        for t in range(PACK): stage1(0, t)
+        pick(0)
+        first_weights(0)
+        first_weights(1)
+        pick(1)
+        for t in range(PACK): stage1(1, t)
+        combine(0)
+        packed_weights()
+        left_weights(0)
+        multiply(0)
+        combine(1)
+        multiply(1)
+        pick(2)
+        left_weights(1)
+        pick(3)
+        combine(2)
+        multiply(2)
+        pick(4)
+        combine(3)
+        multiply(3)
+        combine(4)
+        multiply(4)
 
         for q in range(4):
             engine = nc.sync if q % 2 == 0 else nc.scalar

@@ -21,17 +21,13 @@ PACK = 4
 PASS = P * PACK
 BANK = 512
 QUARTER = 128
+LIST_GROUP = 16
+SECOND_ROWS = 16
+
 CHUNKS = ((0, 0, 256), (0, 256, 256), (1, 0, 256), (1, 256, 128), (1, 384, 128))
-H2_SLOTS = ("a2", "slot0", "a2", "slot0", "a2")
-H1_SLOTS = ("a1", "slot1", "a1", "slot1", "a1")
-T_MAJOR = (0, 2)
-SCALAR_COLS = 224
-BENT_SCALAR = ()
-WEAVE_SCALAR = ()
-GAP_G = ()
-BENT_G = ()
-Y_SCALAR = (0,)
-WA_ENG = ("scalar", "scalar")
+H2_TAGS = ("picked2", "rows_a")
+H1_TAGS = ("picked1", "rounded1")
+SCALAR_COLS = 256
 
 
 def tile_list_otolith_pair_features_kernel(
@@ -42,49 +38,31 @@ def tile_list_otolith_pair_features_kernel(
     with ExitStack() as ctx:
         lists = ctx.enter_context(tc.tile_pool(name="lists", bufs=1))
         keep = ctx.enter_context(tc.tile_pool(name="keep", bufs=1))
-        stage = ctx.enter_context(tc.tile_pool(name="stage", bufs=3))
+        ring = ctx.enter_context(tc.tile_pool(name="ring", bufs=2))
         f_psum = ctx.enter_context(tc.psum_pool(name="f_psum", bufs=4))
         y_psum = ctx.enter_context(tc.psum_pool(name="y_psum", bufs=1))
 
-        offs_sb = lists.tile([P, S // 16], U16, name="offs_sb")
-        pos1_sb = lists.tile([P, PAIRS // 16], U16, name="pos1_sb")
-        pos2_sb = lists.tile([P, PAIRS // 16], U16, name="pos2_sb")
+        offs_sb = lists.tile([P, S // LIST_GROUP], U16, name="offs_sb")
+        pos1_sb = lists.tile([P, PAIRS // LIST_GROUP], U16, name="pos1_sb")
+        pos2_sb = lists.tile([P, PAIRS // LIST_GROUP], U16, name="pos2_sb")
 
-        tab_scale_win = keep.tile([P, T], U8, name="tab_scale_win", tag="scale_rows", align_bytes=64)
-        nc.gpsimd.memset(tab_scale_win[:].bitcast(I32), 0)
-        v_scale1 = keep.tile([P, S], U8, name="v_scale1", align_bytes=64)
-        nc.gpsimd.memset(v_scale1[:].bitcast(I32), 0)
-        for r in range(4):
-            nc.scalar.dma_start(
-                out=tab_scale_win[r:P:16, :].bitcast(I32),
-                in_=tab_scales.rearrange("a (q r) t -> r q a t", r=4)[r].bitcast(I32),
-            )
-        gain_sb = keep.tile([P, 2, PACK], F32, name="gain_sb")
-
-        def load_rows(w, row0, col0, width, name, tag):
-            raw = keep.tile([P, PACK, width], F32, name="raw_" + name, tag=tag, align_bytes=64)
+        def load_rows(w, row0, col0, name, tag):
+            raw = keep.tile([P, PACK, PASS], F32, name="raw_" + name, tag=tag, align_bytes=64)
             nc.sync.dma_start(
-                out=raw[:],
-                in_=w[row0 : row0 + PASS, col0 : col0 + width].rearrange("(p j) c -> p j c", j=PACK),
+                out=raw[:], in_=w[row0 : row0 + PASS, col0 : col0 + PASS].rearrange("(p j) c -> p j c", j=PACK)
             )
             return raw
 
-        def cast_rows(engine, grouped, raw, m0):
-            width = raw.shape[2]
-            dst = grouped[:].rearrange("p (t m j) -> p m j t", t=PACK, j=PACK)[:, m0 : m0 + width // PACK]
-            src = raw.rearrange("p j (m t) -> p m j t", t=PACK)
-            if engine == "scalar":
-                nc.scalar.copy(out=dst, in_=src)
-            elif engine == "gpsimd":
-                for m in range(0, width // PACK, 32):
-                    nc.gpsimd.tensor_scalar(
-                        out=dst[:, m : m + 32], in0=src[:, m : m + 32], scalar1=1.0, scalar2=0.0, op0=ALU.mult, op1=ALU.add
-                    )
-            else:
-                nc.vector.tensor_copy(out=dst, in_=src)
+        def rounded_tile(name, tag):
+            return keep.tile([P, PASS * PACK], BF16, name=name, tag=tag, align_bytes=64)
 
-        def quantize(grouped, name, parts=1):
-            width = grouped.shape[1] // PACK
+        def round_and_deal(copy, rounded, raw, col0, col1):
+            dst = rounded[:].rearrange("p (u e m j) -> p u m j e", u=2, e=2, j=PACK)
+            src = raw[:, :, col0:col1].rearrange("p j (m u e) -> p u m j e", u=2, e=2)
+            copy(out=dst[:, :, col0 // PACK : col1 // PACK], in_=src)
+
+        def quantize(rounded, name, parts=1):
+            width = rounded.shape[1] // PACK
             codes = keep.tile([P, width], U32, name=name + "_codes", align_bytes=64)
             scales = keep.tile([P, width], U8, name=name + "_scales", align_bytes=64)
             step = width // parts
@@ -92,41 +70,55 @@ def tile_list_otolith_pair_features_kernel(
                 nc.vector.quantize_mx(
                     out=codes[:, c : c + step].bitcast(FP8X4),
                     scales=scales[:, c : c + step],
-                    in_=grouped[:, PACK * c : PACK * (c + step)],
+                    in_=rounded[:, PACK * c : PACK * (c + step)],
                 )
             return codes, scales
 
-        def weight_group(name, tag):
-            return keep.tile([P, PASS * PACK], BF16, name=name, tag=tag, align_bytes=64)
+        def weave_src(ap):
+            return ap.rearrange("p t (c i) -> p c t i", i=4)
 
+        def weave_dst(ap):
+            return ap.rearrange("p (c i t) -> p c t i", i=4, t=PACK)
+
+        tab_scale_win = keep.tile([P, T], U8, name="tab_scale_win", tag="scale_rows", align_bytes=64)
+        nc.gpsimd.memset(tab_scale_win[:].bitcast(I32), 0)
+        v_scale1 = keep.tile([P, S], U8, name="v_scale1", align_bytes=64)
+        nc.gpsimd.memset(v_scale1[:].bitcast(I32), 0)
+        for r in range(4):
+            nc.scalar.dma_start(
+                out=tab_scale_win[r:P:SECOND_ROWS, :].bitcast(I32),
+                in_=tab_scales.rearrange("a (q r) t -> r q a t", r=4)[r].bitcast(I32),
+            )
+
+        gain_sb = keep.tile([P, 2, PACK], F32, name="gain_sb")
+        tab_win = [keep.tile([P, T], U16, name="tab_win%d" % a, tag="words%d" % a, align_bytes=64) for a in range(2)]
         nc.sync.dma_start(offs_sb[:], offs)
         nc.sync.dma_start(out=gain_sb[:], in_=gain.rearrange("(b p t) -> p b t", b=2, t=PACK))
-        tab_win = []
-        for a in range(2):
-            tab_win.append(keep.tile([P, T], U16, name="tab_win%d" % a, tag="words%d" % a, align_bytes=64))
         nc.sync.dma_start(out=tab_win[0][:].bitcast(I32), in_=tab_words[0].bitcast(I32))
         nc.sync.dma_start(pos2_sb[:], pos2)
         nc.sync.dma_start(pos1_sb[:], pos1)
-        raw00 = load_rows(w1, 0, 0, PASS, "w00", "rows_a")
+        raw00 = load_rows(w1, 0, 0, "w00", "rows_a")
         nc.sync.dma_start(out=tab_win[1][:].bitcast(I32), in_=tab_words[1].bitcast(I32))
-        raw10 = load_rows(w1, PASS, 0, PASS, "w10", "rows_b")
+        raw10 = load_rows(w1, PASS, 0, "w10", "rows_b")
 
         v_words = [keep.tile([P, S], U16, name="v_words%d" % a, align_bytes=64) for a in range(2)]
         v_scale0 = keep.tile([P, S], U8, name="v_scale0", align_bytes=64)
         nc.vector.tensor_copy(v_words[0][:], tab_win[0][:].indirect(offs_sb[:]))
         nc.vector.tensor_copy(v_scale0[:], tab_scale_win[:].indirect(offs_sb[:]))
-        nc.sync.dma_start(out=v_scale1[0:112, :].bitcast(I32), in_=v_scale0[16:P, :].bitcast(I32))
+        nc.sync.dma_start(
+            out=v_scale1[0 : P - SECOND_ROWS, :].bitcast(I32), in_=v_scale0[SECOND_ROWS:P, :].bitcast(I32)
+        )
         nc.vector.tensor_copy(v_words[1][:], tab_win[1][:].indirect(offs_sb[:]))
         v_scales = (v_scale0, v_scale1)
 
         w1_q = {}
-        grouped = weight_group("g00", "slot0")
-        cast_rows("scalar", grouped, raw00[:], 0)
-        w1_q[0, 0] = quantize(grouped, "w00")
-        grouped = weight_group("g10", "slot1")
-        cast_rows("scalar", grouped, raw10[:, :, 0:SCALAR_COLS], 0)
-        cast_rows("vector", grouped, raw10[:, :, SCALAR_COLS:PASS], SCALAR_COLS // PACK)
-        w1_q[1, 0] = quantize(grouped, "w10", PACK)
+        rounded = rounded_tile("r00", "rounded0")
+        round_and_deal(nc.scalar.copy, rounded, raw00, 0, PASS)
+        w1_q[0, 0] = quantize(rounded, "w00")
+        rounded = rounded_tile("r10", "rounded1")
+        round_and_deal(nc.scalar.copy, rounded, raw10, 0, SCALAR_COLS)
+        round_and_deal(nc.vector.tensor_copy, rounded, raw10, SCALAR_COLS, PASS)
+        w1_q[1, 0] = quantize(rounded, "w10", parts=PACK)
 
         inv_gain = keep.tile([P, 2, PACK], F32, name="inv_gain")
         safe_gain = keep.tile([P, 2, PACK], F32, name="safe_gain")
@@ -154,28 +146,28 @@ def tile_list_otolith_pair_features_kernel(
                         start=(a == 0),
                         stop=(a == 1),
                     )
-            for half in range(2):
-                dst = h[b, t][:, half * BANK : (half + 1) * BANK]
-                if (b, t, half) == (0, 0, 1):
-                    nc.vector.tensor_scalar(
-                        out=dst, in0=banks[half][:], scalar1=gain_sb[:, b, t : t + 1], scalar2=None, op0=ALU.mult
-                    )
-                else:
-                    nc.scalar.activation(out=dst, in_=banks[half][:], func=ACT.Copy, scale=gain_sb[:, b, t : t + 1])
+            gain_col = gain_sb[:, b, t : t + 1]
+            nc.scalar.activation(out=h[b, t][:, 0:BANK], in_=banks[0][:], func=ACT.Copy, scale=gain_col)
+            if (b, t) == (0, 0):
+                nc.vector.tensor_scalar(
+                    out=h[b, t][:, BANK:S], in0=banks[1][:], scalar1=gain_col, scalar2=None, op0=ALU.mult
+                )
+            else:
+                nc.scalar.activation(out=h[b, t][:, BANK:S], in_=banks[1][:], func=ACT.Copy, scale=gain_col)
+
+        def w1_second_half(a):
+            raw = load_rows(w1, a * PASS, PASS, "w%d1" % a, ("scale_rows", "rows_a")[a])
+            rounded = rounded_tile("r%d1" % a, "rounded%d" % a)
+            round_and_deal(nc.scalar.copy, rounded, raw, 0, PASS)
+            w1_q[a, 1] = quantize(rounded, "w%d1" % a)
 
         wa_q = {}
 
-        def first_weights(a):
-            raw = load_rows(w1, a * PASS, PASS, PASS, "w%d1" % a, ("scale_rows", "rows_a")[a])
-            grouped = weight_group("g%d1" % a, "slot%d" % a)
-            cast_rows("scalar", grouped, raw[:], 0)
-            w1_q[a, 1] = quantize(grouped, "w%d1" % a)
-
-        def left_weights(b):
-            raw = load_rows(wa, b * PASS, 0, N, "wa%d" % b, ("scale_rows", "rows_a")[b])
-            grouped = weight_group("ga%d" % b, "slot_wa")
-            cast_rows(WA_ENG[b], grouped, raw[:], 0)
-            wa_q[b] = quantize(grouped, "wa%d" % b)
+        def wa_pass(b):
+            raw = load_rows(wa, b * PASS, 0, "wa%d" % b, ("scale_rows", "words1")[b])
+            rounded = rounded_tile("ra%d" % b, "rounded_wa")
+            round_and_deal(nc.scalar.copy, rounded, raw, 0, PASS)
+            wa_q[b] = quantize(rounded, "wa%d" % b)
 
         wc_codes = keep.tile([P, 2, N], I32, name="wc_codes", align_bytes=64)
         wb_codes = keep.tile([P, 2, N], U16, name="wb_codes", align_bytes=64)
@@ -192,10 +184,10 @@ def tile_list_otolith_pair_features_kernel(
             )
             wbc_rows = keep.tile([P, 2, N], U8, name="wbc_rows", tag="rows_b", align_bytes=64)
             nc.gpsimd.memset(wbc_rows[:].bitcast(I32), 0)
-            for k, rows in ((0, wb_scales), (4, wc_scales)):
+            for first, rows in ((0, wb_scales), (4, wc_scales)):
                 for q in range(4):
                     nc.sync.dma_start(
-                        out=wbc_rows[32 * q + k : 32 * q + k + 4].bitcast(I32),
+                        out=wbc_rows[32 * q + first : 32 * q + first + 4].bitcast(I32),
                         in_=rows[:, 4 * q : 4 * q + 4, :].rearrange("a r c -> r a c").bitcast(I32),
                     )
             nc.vector.tensor_copy(
@@ -220,120 +212,107 @@ def tile_list_otolith_pair_features_kernel(
         y_scales = keep.tile([P, PAIRS], U8, name="y_scales", align_bytes=64)
         y_rows = out_0.rearrange("(p t) j -> p t j", t=PACK)
         y_words = out_1[0].rearrange("p m t -> p (m t)").bitcast(I32)
-
-        def walk_src(ap):
-            return ap.rearrange("p t (c i) -> p c t i", i=4)
-
-        def walk_dst(ap):
-            return ap.rearrange("p (c i t) -> p c t i", i=4, t=PACK)
-
-        def stage2(which, b, j0, operand):
-            codes, scales = operand
-            for c0 in range(0, codes.shape[1], QUARTER):
-                bank = y_banks[(j0 + c0) // QUARTER]
-                for t in range(PACK):
-                    lhsT, lhsT_scale = stationary(which, b, t)
-                    nc.tensor.matmul_mx(
-                        out=bank[:, t, :],
-                        lhsT=lhsT,
-                        lhsT_scale=lhsT_scale,
-                        rhs=codes[:, c0 : c0 + QUARTER].bitcast(FP8X4),
-                        rhs_scale=scales[:, c0 : c0 + QUARTER],
-                        start=(b == 0 and which == "bent" and t == 0),
-                        stop=(b == 1 and which == "diff" and t == PACK - 1),
-                    )
-
-        def finish(q):
-            j = slice(q * QUARTER, (q + 1) * QUARTER)
-            y = keep.tile([P, PACK, QUARTER], F32, name="y%d" % q, tag="y", bufs=2)
-            nc.scalar.copy(out=y[:], in_=y_banks[q][:])
-            nc.sync.dma_start(out=y_rows[:, :, j], in_=y[:])
-            y_grouped = keep.tile([P, PACK * QUARTER], BF16, name="y_grouped%d" % q, tag="y_grouped", bufs=2, align_bytes=64)
-            if q in Y_SCALAR:
-                nc.scalar.copy(out=walk_dst(y_grouped[:]), in_=walk_src(y[:]))
-            else:
-                nc.vector.tensor_copy(out=walk_dst(y_grouped[:]), in_=walk_src(y[:]))
-            nc.vector.quantize_mx(out=y_codes[:, j].bitcast(FP8X4), scales=y_scales[:, j], in_=y_grouped[:])
-            nc.sync.dma_start(out=y_words[:, j], in_=y_codes[:, j].bitcast(I32))
-
         picked = {}
-        GAP_ENG = lambda n: nc.gpsimd if n in GAP_G else nc.vector
-        BENT_ENG = lambda n: nc.gpsimd if n in BENT_G else nc.vector
+        operands = {}
 
         def pick(n):
             b, j0, width = CHUNKS[n]
-            entries = slice(j0 // 16, (j0 + width) // 16)
-            h2 = keep.tile([P, PACK, width], F32, name="h2_%d" % n, tag=H2_SLOTS[n], align_bytes=64)
-            h1 = keep.tile([P, PACK, width], F32, name="h1_%d" % n, tag=H1_SLOTS[n], align_bytes=64)
-            order = [(w, t) for t in range(PACK) for w in (2, 1)] if n in T_MAJOR else [(w, t) for w in (2, 1) for t in range(PACK)]
-            for w, t in order:
-                dst, pos = (h2, pos2_sb) if w == 2 else (h1, pos1_sb)
+            entries = slice(j0 // LIST_GROUP, (j0 + width) // LIST_GROUP)
+            h2 = keep.tile([P, PACK, width], F32, name="h2_%d" % n, tag=H2_TAGS[n % 2], align_bytes=64)
+            h1 = keep.tile([P, PACK, width], F32, name="h1_%d" % n, tag=H1_TAGS[n % 2], align_bytes=64)
+            gap = ring.tile([P, PACK, width], F32, name="gap_%d" % n, tag="gap")
+            lookups = ((h2, pos2_sb), (h1, pos1_sb))
+            if j0 == 0:
+                order = [(lookup, t) for t in range(PACK) for lookup in lookups]
+            else:
+                order = [(lookup, t) for lookup in lookups for t in range(PACK)]
+            for (dst, pos), t in order:
                 nc.vector.tensor_copy(dst[:, t, :], h[b, t][:].indirect(pos[:, entries]))
-            gap = stage.tile([P, PACK, width], F32, name="gap_%d" % n, tag="gap", bufs=2)
-            GAP_ENG(n).tensor_tensor(out=gap[:], in0=h1[:], in1=h2[:], op=ALU.subtract)
+            nc.vector.tensor_tensor(out=gap[:], in0=h1[:], in1=h2[:], op=ALU.subtract)
             picked[n] = (h1, h2, gap)
-
-        made = {}
 
         def combine(n):
             b, j0, width = CHUNKS[n]
             h1, h2, gap = picked[n]
-            bounded = stage.tile([P, PACK, width], F32, name="bounded_%d" % n, tag="bounded", bufs=2)
-            left = stage.tile([P, PACK * width], BF16, name="left_%d" % n, tag="left", bufs=2, align_bytes=64)
-            bent = stage.tile([P, PACK * width], BF16, name="bent_%d" % n, tag="bent", bufs=2, align_bytes=64)
-            diff = stage.tile([P, PACK * width], BF16, name="diff_%d" % n, tag="diff", bufs=2, align_bytes=64)
+            bounded = ring.tile([P, PACK, width], F32, name="bounded_%d" % n, tag="bounded")
+            left = ring.tile([P, PACK * width], BF16, name="left_%d" % n, tag="left", align_bytes=64)
+            bent = ring.tile([P, PACK * width], BF16, name="bent_%d" % n, tag="bent", align_bytes=64)
+            diff = ring.tile([P, PACK * width], BF16, name="diff_%d" % n, tag="diff", align_bytes=64)
             for t in range(PACK):
                 nc.scalar.activation(
                     out=bounded[:, t, :], in_=h2[:, t, :], func=ACT.Tanh, scale=inv_gain[:, b, t : t + 1]
                 )
-            nc.scalar.copy(out=walk_dst(left[:]), in_=walk_src(h1[:]))
-            nc.scalar.activation(out=walk_dst(diff[:]), in_=walk_src(gap[:]), func=ACT.Abs)
-            if n in BENT_SCALAR:
-                rows = stage.tile([P, PACK, width], BF16, name="bent_rows_%d" % n, tag="bent_rows", bufs=2)
+            nc.scalar.copy(out=weave_dst(left[:]), in_=weave_src(h1[:]))
+            nc.scalar.activation(out=weave_dst(diff[:]), in_=weave_src(gap[:]), func=ACT.Abs)
+            if b == 0:
+                rows = ring.tile([P, PACK, width], BF16, name="bent_rows_%d" % n, tag="bent_rows")
                 for t in range(PACK):
-                    nc.scalar.activation(out=rows[:, t, :], in_=bounded[:, t, :], func=ACT.Copy, scale=gain_sb[:, b, t : t + 1])
-                if n in WEAVE_SCALAR:
-                    nc.scalar.copy(out=walk_dst(bent[:]), in_=walk_src(rows[:]))
-                else:
-                    nc.vector.tensor_copy(out=walk_dst(bent[:]), in_=walk_src(rows[:]))
+                    nc.scalar.activation(
+                        out=rows[:, t, :], in_=bounded[:, t, :], func=ACT.Copy, scale=gain_sb[:, b, t : t + 1]
+                    )
+                nc.vector.tensor_copy(out=weave_dst(bent[:]), in_=weave_src(rows[:]))
             else:
                 gains = gain_sb[:, b, :].unsqueeze(1).unsqueeze(3).to_broadcast([P, width // 4, PACK, 4])
-                BENT_ENG(n).tensor_tensor(out=walk_dst(bent[:]), in0=walk_src(bounded[:]), in1=gains, op=ALU.mult)
-            made[n] = [(which, quantize(grouped, "%s_%d" % (which, n))) for which, grouped in (("bent", bent), ("left", left), ("diff", diff))]
+                nc.vector.tensor_tensor(out=weave_dst(bent[:]), in0=weave_src(bounded[:]), in1=gains, op=ALU.mult)
+            operands[n] = [
+                (which, quantize(woven, "%s_%d" % (which, n)))
+                for which, woven in (("bent", bent), ("left", left), ("diff", diff))
+            ]
 
         def multiply(n):
             b, j0, width = CHUNKS[n]
-            for which, operand in made[n]:
-                stage2(which, b, j0, operand)
+            for which, (codes, scales) in operands[n]:
+                for c0 in range(0, width, QUARTER):
+                    for t in range(PACK):
+                        lhsT, lhsT_scale = stationary(which, b, t)
+                        nc.tensor.matmul_mx(
+                            out=y_banks[(j0 + c0) // QUARTER][:, t, :],
+                            lhsT=lhsT,
+                            lhsT_scale=lhsT_scale,
+                            rhs=codes[:, c0 : c0 + QUARTER].bitcast(FP8X4),
+                            rhs_scale=scales[:, c0 : c0 + QUARTER],
+                            start=(b == 0 and which == "bent" and t == 0),
+                            stop=(b == 1 and which == "diff" and t == PACK - 1),
+                        )
             if b == 1:
                 for q in range(j0 // QUARTER, (j0 + width) // QUARTER):
                     finish(q)
 
-        for t in range(PACK): stage1(0, t)
+        def finish(q):
+            j = slice(q * QUARTER, (q + 1) * QUARTER)
+            y = ring.tile([P, PACK, QUARTER], F32, name="y%d" % q, tag="y")
+            nc.scalar.copy(out=y[:], in_=y_banks[q][:])
+            nc.sync.dma_start(out=y_rows[:, :, j], in_=y[:])
+            y_woven = ring.tile([P, PACK * QUARTER], BF16, name="y_woven%d" % q, tag="y_woven", align_bytes=64)
+            weave = nc.scalar.copy if q == 0 else nc.vector.tensor_copy
+            weave(out=weave_dst(y_woven[:]), in_=weave_src(y[:]))
+            nc.vector.quantize_mx(out=y_codes[:, j].bitcast(FP8X4), scales=y_scales[:, j], in_=y_woven[:])
+            nc.sync.dma_start(out=y_words[:, j], in_=y_codes[:, j].bitcast(I32))
+
+        for t in range(PACK):
+            stage1(0, t)
         pick(0)
-        first_weights(0)
-        first_weights(1)
+        w1_second_half(0)
+        w1_second_half(1)
         pick(1)
-        for t in range(PACK): stage1(1, t)
+        for t in range(PACK):
+            stage1(1, t)
         combine(0)
         packed_weights()
-        left_weights(0)
+        wa_pass(0)
         multiply(0)
         combine(1)
         multiply(1)
         pick(2)
-        left_weights(1)
-        pick(3)
-        combine(2)
-        multiply(2)
-        pick(4)
-        combine(3)
-        multiply(3)
-        combine(4)
-        multiply(4)
+        wa_pass(1)
+        for n in range(2, len(CHUNKS)):
+            if n + 1 < len(CHUNKS):
+                pick(n + 1)
+            combine(n)
+            multiply(n)
 
         for q in range(4):
-            engine = nc.sync if q % 2 == 0 else nc.scalar
-            engine.dma_start(
+            queue = nc.sync if q % 2 == 0 else nc.scalar
+            queue.dma_start(
                 out=out_2[0, 4 * q : 4 * q + 4, :].bitcast(I32), in_=y_scales[32 * q : 32 * q + 4, :].bitcast(I32)
             )

from contextlib import ExitStack

import concourse.mybir as mybir

K, H, N, T, S, PAIRS = 1024, 1024, 512, 4096, 1024, 512
FLOPS = 2 * K * H * S + 3 * 2 * H * N * PAIRS

F32 = mybir.dt.float32
BF16 = mybir.dt.bfloat16
I32 = mybir.dt.int32
U32 = mybir.dt.uint32
U16 = mybir.dt.uint16
U8 = mybir.dt.uint8
FP8X4 = mybir.dt.float8_e4m3fn_x4
FP4X4 = mybir.dt.float4_e2m1fn_x4
ACT = mybir.ActivationFunctionType
ALU = mybir.AluOpType

P = 128
PACK = 4
PASS = P * PACK
BANK = 512
QUARTER = 128
LIST_GROUP = 16
SECOND_ROWS = 16

CHUNKS = ((0, 0, 256), (0, 256, 256), (1, 0, 256), (1, 256, 128), (1, 384, 128))
H2_TAGS = ("picked2", "rows_a")
H1_TAGS = ("picked1", "rounded1")
SCALAR_COLS = 256


def tile_list_otolith_pair_features_kernel(
    tc, tab_words, tab_scales, offs, pos1, pos2, w1, gain, wa, wb_words, wb_scales, wc_words, wc_scales,
    out_0, out_1, out_2,
):
    nc = tc.nc
    with ExitStack() as ctx:
        lists = ctx.enter_context(tc.tile_pool(name="lists", bufs=1))
        keep = ctx.enter_context(tc.tile_pool(name="keep", bufs=1))
        ring = ctx.enter_context(tc.tile_pool(name="ring", bufs=2))
        f_psum = ctx.enter_context(tc.psum_pool(name="f_psum", bufs=4))
        y_psum = ctx.enter_context(tc.psum_pool(name="y_psum", bufs=1))

        offs_sb = lists.tile([P, S // LIST_GROUP], U16, name="offs_sb")
        pos1_sb = lists.tile([P, PAIRS // LIST_GROUP], U16, name="pos1_sb")
        pos2_sb = lists.tile([P, PAIRS // LIST_GROUP], U16, name="pos2_sb")

        def load_rows(w, row0, col0, name, tag):
            raw = keep.tile([P, PACK, PASS], F32, name="raw_" + name, tag=tag, align_bytes=64)
            nc.sync.dma_start(
                out=raw[:], in_=w[row0 : row0 + PASS, col0 : col0 + PASS].rearrange("(p j) c -> p j c", j=PACK)
            )
            return raw

        def rounded_tile(name, tag):
            return keep.tile([P, PASS * PACK], BF16, name=name, tag=tag, align_bytes=64)

        def round_and_deal(copy, rounded, raw, col0, col1):
            dst = rounded[:].rearrange("p (u e m j) -> p u m j e", u=2, e=2, j=PACK)
            src = raw[:, :, col0:col1].rearrange("p j (m u e) -> p u m j e", u=2, e=2)
            copy(out=dst[:, :, col0 // PACK : col1 // PACK], in_=src)

        def quantize(rounded, name, parts=1):
            width = rounded.shape[1] // PACK
            codes = keep.tile([P, width], U32, name=name + "_codes", align_bytes=64)
            scales = keep.tile([P, width], U8, name=name + "_scales", align_bytes=64)
            step = width // parts
            for c in range(0, width, step):
                nc.vector.quantize_mx(
                    out=codes[:, c : c + step].bitcast(FP8X4),
                    scales=scales[:, c : c + step],
                    in_=rounded[:, PACK * c : PACK * (c + step)],
                )
            return codes, scales

        def weave_src(ap):
            return ap.rearrange("p t (c i) -> p c t i", i=4)

        def weave_dst(ap):
            return ap.rearrange("p (c i t) -> p c t i", i=4, t=PACK)

        tab_scale_win = keep.tile([P, T], U8, name="tab_scale_win", tag="scale_rows", align_bytes=64)
        nc.gpsimd.memset(tab_scale_win[:].bitcast(I32), 0)
        v_scale1 = keep.tile([P, S], U8, name="v_scale1", align_bytes=64)
        nc.gpsimd.memset(v_scale1[:].bitcast(I32), 0)
        for r in range(4):
            nc.scalar.dma_start(
                out=tab_scale_win[r:P:SECOND_ROWS, :].bitcast(I32),
                in_=tab_scales.rearrange("a (q r) t -> r q a t", r=4)[r].bitcast(I32),
            )

        gain_sb = keep.tile([P, 2, PACK], F32, name="gain_sb")
        tab_win = [keep.tile([P, T], U16, name="tab_win%d" % a, tag="words%d" % a, align_bytes=64) for a in range(2)]
        nc.sync.dma_start(offs_sb[:], offs)
        nc.sync.dma_start(out=gain_sb[:], in_=gain.rearrange("(b p t) -> p b t", b=2, t=PACK))
        nc.sync.dma_start(out=tab_win[0][:].bitcast(I32), in_=tab_words[0].bitcast(I32))
        nc.sync.dma_start(pos2_sb[:], pos2)
        nc.sync.dma_start(pos1_sb[:], pos1)
        raw00 = load_rows(w1, 0, 0, "w00", "rows_a")
        nc.sync.dma_start(out=tab_win[1][:].bitcast(I32), in_=tab_words[1].bitcast(I32))
        raw10 = load_rows(w1, PASS, 0, "w10", "rows_b")

        v_words = [keep.tile([P, S], U16, name="v_words%d" % a, align_bytes=64) for a in range(2)]
        v_scale0 = keep.tile([P, S], U8, name="v_scale0", align_bytes=64)
        nc.vector.tensor_copy(v_words[0][:], tab_win[0][:].indirect(offs_sb[:]))
        nc.vector.tensor_copy(v_scale0[:], tab_scale_win[:].indirect(offs_sb[:]))
        nc.sync.dma_start(
            out=v_scale1[0 : P - SECOND_ROWS, :].bitcast(I32), in_=v_scale0[SECOND_ROWS:P, :].bitcast(I32)
        )
        nc.vector.tensor_copy(v_words[1][:], tab_win[1][:].indirect(offs_sb[:]))
        v_scales = (v_scale0, v_scale1)

        w1_q = {}
        rounded = rounded_tile("r00", "rounded0")
        round_and_deal(nc.scalar.copy, rounded, raw00, 0, PASS)
        w1_q[0, 0] = quantize(rounded, "w00")
        rounded = rounded_tile("r10", "rounded1")
        round_and_deal(nc.scalar.copy, rounded, raw10, 0, SCALAR_COLS)
        round_and_deal(nc.vector.tensor_copy, rounded, raw10, SCALAR_COLS, PASS)
        w1_q[1, 0] = quantize(rounded, "w10", parts=PACK)

        inv_gain = keep.tile([P, 2, PACK], F32, name="inv_gain")
        safe_gain = keep.tile([P, 2, PACK], F32, name="safe_gain")
        nc.vector.scalar_tensor_tensor(
            out=safe_gain[:], in0=gain_sb[:], scalar=0.0, in1=gain_sb[:], op0=ALU.is_equal, op1=ALU.add
        )
        nc.vector.reciprocal(out=inv_gain[:], in_=safe_gain[:])

        h = {}

        def stage1(b, t):
            h[b, t] = keep.tile([P, S], F32, name="h%d%d" % (b, t))
            banks = [f_psum.tile([P, BANK], F32, name="f_bank") for half in range(2)]
            cols = slice(t * P, (t + 1) * P)
            for a in range(2):
                codes, scales = w1_q[a, b]
                for half in range(2):
                    m = slice(half * BANK, (half + 1) * BANK)
                    nc.tensor.matmul_mx(
                        out=banks[half][:],
                        lhsT=codes[:, cols].bitcast(FP8X4),
                        lhsT_scale=scales[:, cols],
                        rhs=v_words[a][:, m].bitcast(FP4X4),
                        rhs_scale=v_scales[a][:, m],
                        start=(a == 0),
                        stop=(a == 1),
                    )
            gain_col = gain_sb[:, b, t : t + 1]
            nc.scalar.activation(out=h[b, t][:, 0:BANK], in_=banks[0][:], func=ACT.Copy, scale=gain_col)
            if (b, t) == (0, 0):
                nc.vector.tensor_scalar(
                    out=h[b, t][:, BANK:S], in0=banks[1][:], scalar1=gain_col, scalar2=None, op0=ALU.mult
                )
            else:
                nc.scalar.activation(out=h[b, t][:, BANK:S], in_=banks[1][:], func=ACT.Copy, scale=gain_col)

        def w1_second_half(a):
            raw = load_rows(w1, a * PASS, PASS, "w%d1" % a, ("scale_rows", "rows_a")[a])
            rounded = rounded_tile("r%d1" % a, "rounded%d" % a)
            round_and_deal(nc.scalar.copy, rounded, raw, 0, PASS)
            w1_q[a, 1] = quantize(rounded, "w%d1" % a)

        wa_q = {}

        def wa_pass(b):
            raw = load_rows(wa, b * PASS, 0, "wa%d" % b, ("scale_rows", "words1")[b])
            rounded = rounded_tile("ra%d" % b, "rounded_wa")
            round_and_deal(nc.scalar.copy, rounded, raw, 0, PASS)
            wa_q[b] = quantize(rounded, "wa%d" % b)

        wc_codes = keep.tile([P, 2, N], I32, name="wc_codes", align_bytes=64)
        wb_codes = keep.tile([P, 2, N], U16, name="wb_codes", align_bytes=64)
        wbc_scales = keep.tile([P, 2, N], U8, name="wbc_scales", align_bytes=64)

        def packed_weights():
            wc_raw = keep.tile([P, 2, N], I32, name="wc_raw", tag="words1", align_bytes=64)
            nc.sync.dma_start(out=wc_raw[:], in_=wc_words.rearrange("a p c i -> p a (c i)").bitcast(I32))
            wb_raw = keep.tile([P, 2, N], U16, name="wb_raw", tag="rows_b", align_bytes=64)
            nc.sync.dma_start(out=wb_raw[:].bitcast(I32), in_=wb_words.rearrange("a p c -> p a c").bitcast(I32))
            nc.vector.tensor_copy(
                out=wb_codes[:].rearrange("p a (t m) -> p a t m", t=PACK),
                in_=wb_raw[:].rearrange("p a (m t) -> p a t m", t=PACK),
            )
            wbc_rows = keep.tile([P, 2, N], U8, name="wbc_rows", tag="rows_b", align_bytes=64)
            nc.gpsimd.memset(wbc_rows[:].bitcast(I32), 0)
            for first, rows in ((0, wb_scales), (4, wc_scales)):
                for q in range(4):
                    nc.sync.dma_start(
                        out=wbc_rows[32 * q + first : 32 * q + first + 4].bitcast(I32),
                        in_=rows[:, 4 * q : 4 * q + 4, :].rearrange("a r c -> r a c").bitcast(I32),
                    )
            nc.vector.tensor_copy(
                out=wc_codes[:].rearrange("p a (t c i) -> p a c t i", t=PACK, i=4),
                in_=wc_raw[:].rearrange("p a (c i t) -> p a c t i", t=PACK, i=4),
            )
            nc.vector.tensor_copy(
                out=wbc_scales[:].rearrange("p a (t m) -> p a t m", t=PACK),
                in_=wbc_rows[:].rearrange("p a (m t) -> p a t m", t=PACK),
            )

        def stationary(which, b, t):
            cols = slice(t * P, (t + 1) * P)
            if which == "left":
                return wa_q[b][0][:, cols].bitcast(FP8X4), wa_q[b][1][:, cols]
            if which == "bent":
                return wb_codes[:, b, cols].bitcast(FP4X4), wbc_scales[:, b, cols]
            return wc_codes[:, b, cols].bitcast(FP8X4), wbc_scales[4:P, b, cols]

        y_banks = [y_psum.tile([P, PACK, QUARTER], F32, name="y_bank%d" % q) for q in range(PAIRS // QUARTER)]
        y_codes = keep.tile([P, PAIRS], U32, name="y_codes", align_bytes=64)
        y_scales = keep.tile([P, PAIRS], U8, name="y_scales", align_bytes=64)
        y_rows = out_0.rearrange("(p t) j -> p t j", t=PACK)
        y_words = out_1[0].rearrange("p m t -> p (m t)").bitcast(I32)
        picked = {}
        operands = {}

        def pick(n):
            b, j0, width = CHUNKS[n]
            entries = slice(j0 // LIST_GROUP, (j0 + width) // LIST_GROUP)
            h2 = keep.tile([P, PACK, width], F32, name="h2_%d" % n, tag=H2_TAGS[n % 2], align_bytes=64)
            h1 = keep.tile([P, PACK, width], F32, name="h1_%d" % n, tag=H1_TAGS[n % 2], align_bytes=64)
            gap = ring.tile([P, PACK, width], F32, name="gap_%d" % n, tag="gap")
            lookups = ((h2, pos2_sb), (h1, pos1_sb))
            if j0 == 0:
                order = [(lookup, t) for t in range(PACK) for lookup in lookups]
            else:
                order = [(lookup, t) for lookup in lookups for t in range(PACK)]
            for (dst, pos), t in order:
                nc.vector.tensor_copy(dst[:, t, :], h[b, t][:].indirect(pos[:, entries]))
            nc.vector.tensor_tensor(out=gap[:], in0=h1[:], in1=h2[:], op=ALU.subtract)
            picked[n] = (h1, h2, gap)

        def combine(n):
            b, j0, width = CHUNKS[n]
            h1, h2, gap = picked[n]
            bounded = ring.tile([P, PACK, width], F32, name="bounded_%d" % n, tag="bounded")
            left = ring.tile([P, PACK * width], BF16, name="left_%d" % n, tag="left", align_bytes=64)
            bent = ring.tile([P, PACK * width], BF16, name="bent_%d" % n, tag="bent", align_bytes=64)
            diff = ring.tile([P, PACK * width], BF16, name="diff_%d" % n, tag="diff", align_bytes=64)
            for t in range(PACK):
                nc.scalar.activation(
                    out=bounded[:, t, :], in_=h2[:, t, :], func=ACT.Tanh, scale=inv_gain[:, b, t : t + 1]
                )
            nc.scalar.copy(out=weave_dst(left[:]), in_=weave_src(h1[:]))
            nc.scalar.activation(out=weave_dst(diff[:]), in_=weave_src(gap[:]), func=ACT.Abs)
            if b == 0:
                rows = ring.tile([P, PACK, width], BF16, name="bent_rows_%d" % n, tag="bent_rows")
                for t in range(PACK):
                    nc.scalar.activation(
                        out=rows[:, t, :], in_=bounded[:, t, :], func=ACT.Copy, scale=gain_sb[:, b, t : t + 1]
                    )
                nc.vector.tensor_copy(out=weave_dst(bent[:]), in_=weave_src(rows[:]))
            else:
                gains = gain_sb[:, b, :].unsqueeze(1).unsqueeze(3).to_broadcast([P, width // 4, PACK, 4])
                nc.vector.tensor_tensor(out=weave_dst(bent[:]), in0=weave_src(bounded[:]), in1=gains, op=ALU.mult)
            operands[n] = [
                (which, quantize(woven, "%s_%d" % (which, n)))
                for which, woven in (("bent", bent), ("left", left), ("diff", diff))
            ]

        def multiply(n):
            b, j0, width = CHUNKS[n]
            for which, (codes, scales) in operands[n]:
                for c0 in range(0, width, QUARTER):
                    for t in range(PACK):
                        lhsT, lhsT_scale = stationary(which, b, t)
                        nc.tensor.matmul_mx(
                            out=y_banks[(j0 + c0) // QUARTER][:, t, :],
                            lhsT=lhsT,
                            lhsT_scale=lhsT_scale,
                            rhs=codes[:, c0 : c0 + QUARTER].bitcast(FP8X4),
                            rhs_scale=scales[:, c0 : c0 + QUARTER],
                            start=(b == 0 and which == "bent" and t == 0),
                            stop=(b == 1 and which == "diff" and t == PACK - 1),
                        )
            if b == 1:
                for q in range(j0 // QUARTER, (j0 + width) // QUARTER):
                    finish(q)

        def finish(q):
            j = slice(q * QUARTER, (q + 1) * QUARTER)
            y = ring.tile([P, PACK, QUARTER], F32, name="y%d" % q, tag="y")
            nc.scalar.copy(out=y[:], in_=y_banks[q][:])
            nc.sync.dma_start(out=y_rows[:, :, j], in_=y[:])
            y_woven = ring.tile([P, PACK * QUARTER], BF16, name="y_woven%d" % q, tag="y_woven", align_bytes=64)
            weave = nc.scalar.copy if q == 0 else nc.vector.tensor_copy
            weave(out=weave_dst(y_woven[:]), in_=weave_src(y[:]))
            nc.vector.quantize_mx(out=y_codes[:, j].bitcast(FP8X4), scales=y_scales[:, j], in_=y_woven[:])
            nc.sync.dma_start(out=y_words[:, j], in_=y_codes[:, j].bitcast(I32))

        for t in range(PACK):
            stage1(0, t)
        pick(0)
        w1_second_half(0)
        w1_second_half(1)
        pick(1)
        for t in range(PACK):
            stage1(1, t)
        combine(0)
        packed_weights()
        wa_pass(0)
        multiply(0)
        combine(1)
        multiply(1)
        pick(2)
        wa_pass(1)
        for n in range(2, len(CHUNKS)):
            if n + 1 < len(CHUNKS):
                pick(n + 1)
            combine(n)
            multiply(n)

        for q in range(4):
            queue = nc.sync if q % 2 == 0 else nc.scalar
            queue.dma_start(
                out=out_2[0, 4 * q : 4 * q + 4, :].bitcast(I32), in_=y_scales[32 * q : 32 * q + 4, :].bitcast(I32)
            )
